import numpy as np
CORES = [88,96,104,112,120,216,224,232,240,248]
N = 10
C, TIMES = 128, 3
def setup_inputs(rng):
    return {"x": np.exp(rng.standard_normal((N, 128, C), dtype=np.float32))}
def setup_inputs_big(rng):
    d = setup_inputs(rng)
    for k in ("x",): d[k] = (d[k].astype(np.float32) * 1048576.0).astype(d[k].dtype)
    return d
def setup_inputs_small(rng):
    d = setup_inputs(rng)
    for k in ("x",): d[k] = (d[k].astype(np.float32) * (1 / 1048576.0)).astype(d[k].dtype)
    return d
def setup_inputs_mixed(rng):
    d = setup_inputs(rng)
    f = (10.0 ** rng.uniform(-3, 3, (1, 1, C))).astype(np.float32)
    for k in ("x",): d[k] = (d[k].astype(np.float32) * f).astype(d[k].dtype)
    return d
def reference(x):
    X = x.astype(np.float64)
    for _ in range(TIMES):
        X = X / X.sum(axis=2, keepdims=True)
        X = X / X.sum(axis=(0, 1), keepdims=True)
    return {"y": X.astype(np.float32)}

@@ -1,0 +1,252 @@
+from concourse.bass import DstId, RemoteDMATransfer
+from concourse.mybir import AluOpType, AxisListType, ActivationFunctionType
+
+NSIM = 256
+NR = 10
+Q = 2
+S = NR // Q
+C = 128
+
+SCRATCH = {
+    "xs": ("sbuf", [128, Q * C], "float32"),
+    "xt": ("sbuf", [128, Q * C], "float32"),
+    "ones": ("sbuf", [128, C], "float32"),
+    "ident": ("sbuf", [128, C], "float32"),
+    "dg": ("sbuf", [128, C], "float32"),
+    "yo": ("sbuf", [128, C], "float32"),
+    "land1": ("sbuf", [128, 4 * S], "float32"),
+    "land2": ("sbuf", [128, 4 * S], "float32"),
+    "land3": ("sbuf", [128, 2 * S], "float32"),
+    "snd3": ("sbuf", [128, 2], "float32"),
+    "rs": ("sbuf", [128, 4], "float32"),
+    "av": ("sbuf", [128, 8], "float32"),
+    "cs": ("sbuf", [128, 4], "float32"),
+    "bv": ("sbuf", [128, 4], "float32"),
+    "pc": ("psum", [128, 512], "float32"),
+    "pr0": ("psum", [128, 512], "float32"),
+    "pr1": ("psum", [128, 512], "float32"),
+    "pt0": ("psum", [128, 512], "float32"),
+    "pt1": ("psum", [128, 512], "float32"),
+    "py": ("psum", [128, 512], "float32"),
+}
+SEMAPHORES = (
+    ["ld", "st", "ones", "idn", "loc", "arr1", "arr2", "arr3", "cs4", "b4", "dgs", "pys", "yos"]
+    + ["%s%d" % (n, k) for n in ("x", "rs", "t", "xt") for k in range(Q)]
+    + ["%s%d" % (n, r) for n in ("cs", "b", "pc", "snd") for r in (1, 2, 3)]
+    + ["%s%d_%d" % (n, k, r) for n in ("r", "a") for k in range(Q) for r in (1, 2, 3)]
+)
+
+_CACHE = {}
+
+
+def _bits(m):
+    return bin(m).count("1")
+
+
+def _plan(T, topo):
+    if "p" in _CACHE:
+        return _CACHE["p"]
+    cores = [int(c) for c in T.cores]
+    left = list(range(len(cores)))
+    groups = []
+    while left:
+        i = left.pop(0)
+        grp = [i]
+        for k in list(left):
+            if len(grp) < Q and topo.same_plane(cores[i], cores[k]):
+                grp.append(k)
+                left.remove(k)
+        groups.append(grp)
+    helper = {}
+    for r, c in enumerate(cores):
+        cand = [w for w in range(NSIM)
+                if w not in cores and topo.host(w) == topo.host(c) and topo.chip(w) == topo.chip(c)
+                and all(topo.may_write(w, d) for d in cores)]
+        cand.sort(key=lambda w: (topo.die(w) != topo.die(c), w))
+        helper[r] = cand[0]
+    role = {}
+    for s, grp in enumerate(groups):
+        for j, r in enumerate(grp):
+            role[cores[r]] = ("rank", s, j)
+            role[helper[r]] = ("help", s, j)
+    p = {"cores": cores, "groups": groups, "helper": helper, "role": role}
+    _CACHE["p"] = p
+    return p
+
+
+def _block_masks(topo, p, s, i):
+    grp = p["groups"][s]
+    c0 = p["cores"][grp[i]]
+    masks = {}
+    used = 0
+    for j in sorted(range(len(grp)), key=lambda j: j == i):
+        m = topo.mask(c0, p["helper"][grp[j]]) & ~used
+        masks[j] = m
+        used |= m
+    return masks
+
+
+def _mid_dests(p, s, j):
+    return [p["helper"][p["groups"][t][j]] for t in range(S) if t != s]
+
+
+def _last_dests(p, s, j):
+    return [p["cores"][p["groups"][t][j]] for t in range(S)]
+
+
+def _fan_mask(topo, src, dests):
+    m = topo.mask(src, dests[0])
+    for d in dests:
+        m &= topo.mask(src, d)
+    return m
+
+
+def _fan(g, topo, core, src, dests, aps, remote_sem, local_sem):
+    m = _fan_mask(topo, core, dests)
+    where = []
+    for d in dests:
+        rid, pid = topo.addr(d, core)
+        where.append(DstId(rid=rid, pnc=pid))
+    g.remote_dma_fused([RemoteDMATransfer(dst_ids=where, dma_engine_mask=m, remote_sem=remote_sem,
+                                          srcs=[src], dsts=aps, alu_op=0)], local_sem=local_sem)
+    return _bits(m)
+
+
+def _identity(g, T):
+    g.wait_ge(T.sem.ones, 1)
+    g.affine_select(T.ident[:], T.ones[:], [[-1, C]], AluOpType.is_equal, 0.0, 0, 1).then_inc(T.sem.idn, 1)
+
+
+def _rank_core(g, core, T, topo, p, s, j):
+    V, PE, SC, SY, sem = g.vector, g.tensor, g.scalar, g.sync, T.sem
+    grp = p["groups"][s]
+    X0 = T.xs[:, 0:C]
+    SY.dma_start(X0, T.x[:]).then_inc(sem.ld, 16)
+    V.memset(T.ones[:], 1.0).then_inc(sem.ones, 1)
+
+    masks = _block_masks(topo, p, s, j)
+    trs = []
+    sent = 0
+    for jj in range(len(grp)):
+        h = p["helper"][grp[jj]]
+        k = 0 if jj == j else 1
+        rid, pid = topo.addr(h, core)
+        trs.append(RemoteDMATransfer(dst_ids=[DstId(rid=rid, pnc=pid)], dma_engine_mask=masks[jj],
+                                     remote_sem=sem["x%d" % k], src=X0, dst=T.xs[:, k * C:(k + 1) * C]))
+        sent += _bits(masks[jj])
+    g.wait_ge(sem.ld, 16)
+    g.remote_dma_fused(trs, local_sem=sem.loc)
+
+    _identity(g, T)
+    PE.wait_ge(sem.ld, 16)
+    PE.wait_ge(sem.idn, 1)
+    PE.transpose(T.pt0[:, 0:C], X0, T.ident[:]).then_inc(sem.t0, 1)
+    SC.wait_ge(sem.t0, 1)
+    SC.activation(T.xt[:, 0:C], T.pt0[:, 0:C], ActivationFunctionType.Copy).then_inc(sem.xt0, 1)
+
+    n = sum(_bits(_fan_mask(topo, p["helper"][p["groups"][t][j]], _last_dests(p, t, j))) for t in range(S))
+    V.wait_ge(sem.arr3, n)
+    V.tensor_reduce(T.cs[:, 0:1], T.land3[:, 0:2 * S:2], axis=AxisListType.X, op=AluOpType.add).then_inc(sem.cs4, 1)
+    V.wait_ge(sem.cs4, 1)
+    V.reciprocal(T.bv[:, 0:1], T.cs[:, 0:1]).then_inc(sem.b4, 1)
+    V.wait_ge(sem.b4, 1)
+    V.wait_ge(sem.idn, 1)
+    V.tensor_scalar(T.dg[:], T.ident[:], T.bv[:, 0:1], None, AluOpType.mult).then_inc(sem.dgs, 1)
+    PE.wait_ge(sem.dgs, 1)
+    PE.wait_ge(sem.xt0, 1)
+    PE.matmul(T.py[:, 0:C], T.xt[:, 0:C], T.dg[:], start=True, stop=True).then_inc(sem.pys, 1)
+    V.wait_ge(sem.pys, 1)
+    V.tensor_scalar(T.yo[:], T.py[:, 0:C], T.land3[:, 2 * s + 1:2 * s + 2], None, AluOpType.mult).then_inc(sem.yos, 1)
+    SY.wait_ge(sem.yos, 1)
+    SY.dma_start(T.y[:], T.yo[:]).then_inc(sem.st, 16)
+    SY.wait_ge(sem.st, 16)
+    g.wait_ge(sem.loc, sent)
+
+
+def _helper_core(g, core, T, topo, p, s, j):
+    V, PE, SC, sem = g.vector, g.tensor, g.scalar, T.sem
+    grp = p["groups"][s]
+    nb = len(grp)
+    X = [T.xs[:, k * C:(k + 1) * C] for k in range(nb)]
+    XT = [T.xt[:, k * C:(k + 1) * C] for k in range(nb)]
+    PR = [T["pr%d" % k] for k in range(nb)]
+    PT = [T["pt%d" % k] for k in range(nb)]
+    member = [j] + [i for i in range(nb) if i != j]
+    nx = [_bits(_block_masks(topo, p, s, member[k])[j]) for k in range(nb)]
+    sent = 0
+
+    V.memset(T.ones[:], 1.0).then_inc(sem.ones, 1)
+    _identity(g, T)
+
+    def a_col(k, r):
+        if r == 3 and k == 0:
+            return T.snd3[:, 1:2]
+        return T.av[:, 2 * (r - 1) + k:2 * (r - 1) + k + 1]
+
+    for r in (1, 2, 3):
+        if r == 1:
+            for k in range(nb):
+                V.wait_ge(sem["x%d" % k], nx[k])
+                V.tensor_reduce(T.rs[:, k:k + 1], X[k], axis=AxisListType.X, op=AluOpType.add).then_inc(
+                    sem["rs%d" % k], 1)
+                V.wait_ge(sem["rs%d" % k], 1)
+                V.reciprocal(a_col(k, r), T.rs[:, k:k + 1]).then_inc(sem["a%d_%d" % (k, r)], 1)
+        else:
+            land = T["land%d" % (r - 1)]
+            n = sum(_bits(_fan_mask(topo, p["helper"][p["groups"][t][j]], _mid_dests(p, t, j)))
+                    for t in range(S) if t != s)
+            V.wait_ge(sem["arr%d" % (r - 1)], n)
+            V.wait_ge(sem["snd%d" % (r - 1)], 1)
+            V.tensor_reduce(T.cs[:, r:r + 1], land[:, 0:4 * S:4], axis=AxisListType.X, op=AluOpType.add).then_inc(
+                sem["cs%d" % r], 1)
+            V.wait_ge(sem["cs%d" % r], 1)
+            V.reciprocal(T.bv[:, r:r + 1], T.cs[:, r:r + 1]).then_inc(sem["b%d" % r], 1)
+            PE.wait_ge(sem["b%d" % r], 1)
+            for k in range(nb):
+                PE.wait_ge(sem["xt%d" % k], 1)
+                PE.matmul(PR[k][:, r:r + 1], XT[k], T.bv[:, r:r + 1], start=True, stop=True).then_inc(
+                    sem["r%d_%d" % (k, r)], 1)
+            for k in range(nb):
+                V.wait_ge(sem["r%d_%d" % (k, r)], 1)
+                V.reciprocal(a_col(k, r), PR[k][:, r:r + 1]).then_inc(sem["a%d_%d" % (k, r)], 1)
+
+        for k in range(nb):
+            if r == 1:
+                PE.wait_ge(sem["x%d" % k], nx[k])
+            PE.wait_ge(sem["a%d_%d" % (k, r)], 1)
+            mm = PE.matmul(T.pc[:, r:r + 1], X[k], a_col(k, r), start=(k == 0), stop=(k == nb - 1))
+        mm.then_inc(sem["pc%d" % r], 1)
+        V.wait_ge(sem["pc%d" % r], 1)
+        if r < 3:
+            out = T["land%d" % r][:, 4 * s:4 * s + 1]
+            V.tensor_copy(out, T.pc[:, r:r + 1]).then_inc(sem["snd%d" % r], 1)
+            g.wait_ge(sem["snd%d" % r], 1)
+            dests = _mid_dests(p, s, j)
+            sent += _fan(g, topo, core, out, dests, [out for _ in dests], sem["arr%d" % r], sem.loc)
+        else:
+            V.tensor_copy(T.snd3[:, 0:1], T.pc[:, r:r + 1]).then_inc(sem["snd%d" % r], 1)
+            g.wait_ge(sem["snd%d" % r], 1)
+            g.wait_ge(sem["a0_%d" % r], 1)
+            dests = _last_dests(p, s, j)
+            sent += _fan(g, topo, core, T.snd3[:], dests, [T.land3[:, 2 * s:2 * s + 2] for _ in dests],
+                         sem.arr3, sem.loc)
+
+        if r == 1:
+            PE.wait_ge(sem.idn, 1)
+            for k in range(nb):
+                PE.transpose(PT[k][:, 0:C], X[k], T.ident[:]).then_inc(sem["t%d" % k], 1)
+                SC.wait_ge(sem["t%d" % k], 1)
+                SC.activation(XT[k], PT[k][:, 0:C], ActivationFunctionType.Copy).then_inc(sem["xt%d" % k], 1)
+
+    g.wait_ge(sem.loc, sent)
+
+
+def rank_program(g, core, T, topo):
+    p = _plan(T, topo)
+    if core not in p["role"]:
+        return
+    kind, s, j = p["role"][core]
+    if kind == "rank":
+        _rank_core(g, core, T, topo, p, s, j)
+    else:
+        _helper_core(g, core, T, topo, p, s, j)

@@ -6,6 +6,8 @@ NR = 10
 Q = 2
 S = NR // Q
 C = 128
+H = C // 2
+ON_ENGINES = 4
 
 SCRATCH = {
     "xs": ("sbuf", [128, Q * C], "float32"),
@@ -14,6 +16,8 @@ SCRATCH = {
     "ident": ("sbuf", [128, C], "float32"),
     "dg": ("sbuf", [128, C], "float32"),
     "yo": ("sbuf", [128, C], "float32"),
+    "c1": ("sbuf", [128, 1], "float32"),
+    "land0": ("sbuf", [128, Q], "float32"),
     "land1": ("sbuf", [128, 4 * S], "float32"),
     "land2": ("sbuf", [128, 4 * S], "float32"),
     "land3": ("sbuf", [128, 2 * S], "float32"),
@@ -30,8 +34,9 @@ SCRATCH = {
     "py": ("psum", [128, 512], "float32"),
 }
 SEMAPHORES = (
-    ["ld", "st", "ones", "idn", "loc", "arr1", "arr2", "arr3", "cs4", "b4", "dgs", "pys", "yos"]
-    + ["%s%d" % (n, k) for n in ("x", "rs", "t", "xt") for k in range(Q)]
+    ["ld", "st", "ones", "idn", "loc", "arr0", "arr1", "arr2", "arr3", "rs", "cs4", "b4", "dg0", "dg1", "py0", "py1",
+     "yos"]
+    + ["%s%d" % (n, k) for n in ("x", "t", "xt") for k in range(Q)]
     + ["%s%d" % (n, r) for n in ("cs", "b", "pc", "snd") for r in (1, 2, 3)]
     + ["%s%d_%d" % (n, k, r) for n in ("r", "a") for k in range(Q) for r in (1, 2, 3)]
 )
@@ -41,6 +46,17 @@ _CACHE = {}
 
 def _bits(m):
     return bin(m).count("1")
+
+
+def _take(m, n):
+    out = 0
+    e = 0
+    while n and (m >> e):
+        if (m >> e) & 1:
+            out |= 1 << e
+            n -= 1
+        e += 1
+    return out
 
 
 def _plan(T, topo):
@@ -77,13 +93,18 @@ def _plan(T, topo):
 def _block_masks(topo, p, s, i):
     grp = p["groups"][s]
     c0 = p["cores"][grp[i]]
+    off = 0
     masks = {}
-    used = 0
-    for j in sorted(range(len(grp)), key=lambda j: j == i):
-        m = topo.mask(c0, p["helper"][grp[j]]) & ~used
-        masks[j] = m
-        used |= m
+    for j in range(len(grp)):
+        if j != i:
+            masks[j] = topo.mask(c0, p["helper"][grp[j]])
+            off |= masks[j]
+    masks[i] = _take(topo.mask(c0, p["helper"][grp[i]]) & ~off, ON_ENGINES)
     return masks
+
+
+def _site_helpers(p, s):
+    return [p["helper"][r] for r in p["groups"][s]]
 
 
 def _mid_dests(p, s, j):
@@ -124,40 +145,61 @@ def _rank_core(g, core, T, topo, p, s, j):
     SY.dma_start(X0, T.x[:]).then_inc(sem.ld, 16)
     V.memset(T.ones[:], 1.0).then_inc(sem.ones, 1)
 
+    V.wait_ge(sem.ld, 16)
+    V.tensor_reduce(T.rs[:, 0:1], X0, axis=AxisListType.X, op=AluOpType.add).then_inc(sem.rs, 1)
+    V.wait_ge(sem.rs, 1)
+    V.reciprocal(T.av[:, 0:1], T.rs[:, 0:1]).then_inc(sem["a0_1"], 1)
+    PE.wait_ge(sem.ld, 16)
+    PE.wait_ge(sem["a0_1"], 1)
+    PE.matmul(T.pc[:, 0:1], X0, T.av[:, 0:1], start=True, stop=True).then_inc(sem.pc1, 1)
+    V.wait_ge(sem.pc1, 1)
+    V.tensor_copy(T.c1[:, 0:1], T.pc[:, 0:1]).then_inc(sem.snd1, 1)
+
     masks = _block_masks(topo, p, s, j)
-    trs = []
     sent = 0
-    for jj in range(len(grp)):
-        h = p["helper"][grp[jj]]
+
+    def block_to(jj):
         k = 0 if jj == j else 1
-        rid, pid = topo.addr(h, core)
-        trs.append(RemoteDMATransfer(dst_ids=[DstId(rid=rid, pnc=pid)], dma_engine_mask=masks[jj],
-                                     remote_sem=sem["x%d" % k], src=X0, dst=T.xs[:, k * C:(k + 1) * C]))
-        sent += _bits(masks[jj])
+        rid, pid = topo.addr(p["helper"][grp[jj]], core)
+        g.remote_dma(out_ap=T.xs[:, k * C:(k + 1) * C], in_ap=X0, remote_sem=sem["x%d" % k], local_sem=sem.loc,
+                     pid=pid, routing_id=rid, dma_engine_mask=masks[jj])
+        return _bits(masks[jj])
+
     g.wait_ge(sem.ld, 16)
-    g.remote_dma_fused(trs, local_sem=sem.loc)
+    sent += block_to(j)
+    g.wait_ge(sem.snd1, 1)
+    dests = _site_helpers(p, s)
+    sent += _fan(g, topo, core, T.c1[:, 0:1], dests, [T.land0[:, j:j + 1] for _ in dests], sem.arr0, sem.loc)
+    for jj in range(len(grp)):
+        if jj != j:
+            sent += block_to(jj)
 
     _identity(g, T)
-    PE.wait_ge(sem.ld, 16)
     PE.wait_ge(sem.idn, 1)
     PE.transpose(T.pt0[:, 0:C], X0, T.ident[:]).then_inc(sem.t0, 1)
     SC.wait_ge(sem.t0, 1)
     SC.activation(T.xt[:, 0:C], T.pt0[:, 0:C], ActivationFunctionType.Copy).then_inc(sem.xt0, 1)
 
     n = sum(_bits(_fan_mask(topo, p["helper"][p["groups"][t][j]], _last_dests(p, t, j))) for t in range(S))
+    a3 = T.land3[:, 2 * s + 1:2 * s + 2]
+    PY = [T.py, T.pr0]
+    V.wait_ge(sem.idn, 1)
     V.wait_ge(sem.arr3, n)
     V.tensor_reduce(T.cs[:, 0:1], T.land3[:, 0:2 * S:2], axis=AxisListType.X, op=AluOpType.add).then_inc(sem.cs4, 1)
     V.wait_ge(sem.cs4, 1)
     V.reciprocal(T.bv[:, 0:1], T.cs[:, 0:1]).then_inc(sem.b4, 1)
     V.wait_ge(sem.b4, 1)
-    V.wait_ge(sem.idn, 1)
-    V.tensor_scalar(T.dg[:], T.ident[:], T.bv[:, 0:1], None, AluOpType.mult).then_inc(sem.dgs, 1)
-    PE.wait_ge(sem.dgs, 1)
     PE.wait_ge(sem.xt0, 1)
-    PE.matmul(T.py[:, 0:C], T.xt[:, 0:C], T.dg[:], start=True, stop=True).then_inc(sem.pys, 1)
-    V.wait_ge(sem.pys, 1)
-    V.tensor_scalar(T.yo[:], T.py[:, 0:C], T.land3[:, 2 * s + 1:2 * s + 2], None, AluOpType.mult).then_inc(sem.yos, 1)
-    SY.wait_ge(sem.yos, 1)
+    for h in (0, 1):
+        V.tensor_scalar(T.dg[:, h * H:(h + 1) * H], T.ident[:, h * H:(h + 1) * H], T.bv[:, 0:1], None,
+                        AluOpType.mult).then_inc(sem["dg%d" % h], 1)
+        PE.wait_ge(sem["dg%d" % h], 1)
+        PE.matmul(PY[h][:, 0:H], T.xt[:, 0:C], T.dg[:, h * H:(h + 1) * H], start=True, stop=True).then_inc(
+            sem["py%d" % h], 1)
+    for h in (0, 1):
+        V.wait_ge(sem["py%d" % h], 1)
+        V.tensor_scalar(T.yo[:, h * H:(h + 1) * H], PY[h][:, 0:H], a3, None, AluOpType.mult).then_inc(sem.yos, 1)
+    SY.wait_ge(sem.yos, 2)
     SY.dma_start(T.y[:], T.yo[:]).then_inc(sem.st, 16)
     SY.wait_ge(sem.st, 16)
     g.wait_ge(sem.loc, sent)
@@ -183,36 +225,41 @@ def _helper_core(g, core, T, topo, p, s, j):
             return T.snd3[:, 1:2]
         return T.av[:, 2 * (r - 1) + k:2 * (r - 1) + k + 1]
 
-    for r in (1, 2, 3):
-        if r == 1:
-            for k in range(nb):
-                V.wait_ge(sem["x%d" % k], nx[k])
-                V.tensor_reduce(T.rs[:, k:k + 1], X[k], axis=AxisListType.X, op=AluOpType.add).then_inc(
-                    sem["rs%d" % k], 1)
-                V.wait_ge(sem["rs%d" % k], 1)
-                V.reciprocal(a_col(k, r), T.rs[:, k:k + 1]).then_inc(sem["a%d_%d" % (k, r)], 1)
-        else:
-            land = T["land%d" % (r - 1)]
-            n = sum(_bits(_fan_mask(topo, p["helper"][p["groups"][t][j]], _mid_dests(p, t, j)))
-                    for t in range(S) if t != s)
-            V.wait_ge(sem["arr%d" % (r - 1)], n)
-            V.wait_ge(sem["snd%d" % (r - 1)], 1)
-            V.tensor_reduce(T.cs[:, r:r + 1], land[:, 0:4 * S:4], axis=AxisListType.X, op=AluOpType.add).then_inc(
-                sem["cs%d" % r], 1)
-            V.wait_ge(sem["cs%d" % r], 1)
-            V.reciprocal(T.bv[:, r:r + 1], T.cs[:, r:r + 1]).then_inc(sem["b%d" % r], 1)
-            PE.wait_ge(sem["b%d" % r], 1)
-            for k in range(nb):
-                PE.wait_ge(sem["xt%d" % k], 1)
-                PE.matmul(PR[k][:, r:r + 1], XT[k], T.bv[:, r:r + 1], start=True, stop=True).then_inc(
-                    sem["r%d_%d" % (k, r)], 1)
-            for k in range(nb):
-                V.wait_ge(sem["r%d_%d" % (k, r)], 1)
-                V.reciprocal(a_col(k, r), PR[k][:, r:r + 1]).then_inc(sem["a%d_%d" % (k, r)], 1)
+    n0 = sum(_bits(_fan_mask(topo, p["cores"][r], _site_helpers(p, s))) for r in grp)
+    out = T.land1[:, 4 * s:4 * s + 1]
+    V.wait_ge(sem.arr0, n0)
+    V.tensor_reduce(out, T.land0[:, 0:nb], axis=AxisListType.X, op=AluOpType.add).then_inc(sem.snd1, 1)
+    g.wait_ge(sem.snd1, 1)
+    dests = _mid_dests(p, s, j)
+    sent += _fan(g, topo, core, out, dests, [out for _ in dests], sem.arr1, sem.loc)
+
+    PE.wait_ge(sem.idn, 1)
+    for k in range(nb):
+        PE.wait_ge(sem["x%d" % k], nx[k])
+        PE.transpose(PT[k][:, 0:C], X[k], T.ident[:]).then_inc(sem["t%d" % k], 1)
+        SC.wait_ge(sem["t%d" % k], 1)
+        SC.activation(XT[k], PT[k][:, 0:C], ActivationFunctionType.Copy).then_inc(sem["xt%d" % k], 1)
+
+    for r in (2, 3):
+        land = T["land%d" % (r - 1)]
+        n = sum(_bits(_fan_mask(topo, p["helper"][p["groups"][t][j]], _mid_dests(p, t, j)))
+                for t in range(S) if t != s)
+        V.wait_ge(sem["arr%d" % (r - 1)], n)
+        V.wait_ge(sem["snd%d" % (r - 1)], 1)
+        V.tensor_reduce(T.cs[:, r:r + 1], land[:, 0:4 * S:4], axis=AxisListType.X, op=AluOpType.add).then_inc(
+            sem["cs%d" % r], 1)
+        V.wait_ge(sem["cs%d" % r], 1)
+        V.reciprocal(T.bv[:, r:r + 1], T.cs[:, r:r + 1]).then_inc(sem["b%d" % r], 1)
+        PE.wait_ge(sem["b%d" % r], 1)
+        for k in range(nb):
+            PE.wait_ge(sem["xt%d" % k], 1)
+            PE.matmul(PR[k][:, r:r + 1], XT[k], T.bv[:, r:r + 1], start=True, stop=True).then_inc(
+                sem["r%d_%d" % (k, r)], 1)
+        for k in range(nb):
+            V.wait_ge(sem["r%d_%d" % (k, r)], 1)
+            V.reciprocal(a_col(k, r), PR[k][:, r:r + 1]).then_inc(sem["a%d_%d" % (k, r)], 1)
 
         for k in range(nb):
-            if r == 1:
-                PE.wait_ge(sem["x%d" % k], nx[k])
             PE.wait_ge(sem["a%d_%d" % (k, r)], 1)
             mm = PE.matmul(T.pc[:, r:r + 1], X[k], a_col(k, r), start=(k == 0), stop=(k == nb - 1))
         mm.then_inc(sem["pc%d" % r], 1)
@@ -230,13 +277,6 @@ def _helper_core(g, core, T, topo, p, s, j):
             dests = _last_dests(p, s, j)
             sent += _fan(g, topo, core, T.snd3[:], dests, [T.land3[:, 2 * s:2 * s + 2] for _ in dests],
                          sem.arr3, sem.loc)
-
-        if r == 1:
-            PE.wait_ge(sem.idn, 1)
-            for k in range(nb):
-                PE.transpose(PT[k][:, 0:C], X[k], T.ident[:]).then_inc(sem["t%d" % k], 1)
-                SC.wait_ge(sem["t%d" % k], 1)
-                SC.activation(XT[k], PT[k][:, 0:C], ActivationFunctionType.Copy).then_inc(sem["xt%d" % k], 1)
 
     g.wait_ge(sem.loc, sent)
 

@@ -34,8 +34,8 @@ SCRATCH = {
     "py": ("psum", [128, 512], "float32"),
 }
 SEMAPHORES = (
-    ["ld", "st", "ones", "idn", "loc", "arr0", "arr1", "arr2", "arr3", "rs", "cs4", "b4", "dg0", "dg1", "py0", "py1",
-     "yos"]
+    ["ld", "st", "ones", "idn", "idr", "loc", "arr0", "arr1", "arr2", "arr3", "rs", "cs4", "b4", "dg0", "dg1",
+     "py0", "py1", "yos"]
     + ["%s%d" % (n, k) for n in ("x", "t", "xt") for k in range(Q)]
     + ["%s%d" % (n, r) for n in ("cs", "b", "pc", "snd") for r in (1, 2, 3)]
     + ["%s%d_%d" % (n, k, r) for n in ("r", "a") for k in range(Q) for r in (1, 2, 3)]
@@ -122,6 +122,10 @@ def _fan_mask(topo, src, dests):
     return m
 
 
+def _ident_mask(topo, p, s, j):
+    return _fan_mask(topo, p["helper"][p["groups"][s][j]], _mid_dests(p, s, j) + _last_dests(p, s, j))
+
+
 def _fan(g, topo, core, src, dests, aps, remote_sem, local_sem):
     m = _fan_mask(topo, core, dests)
     where = []
@@ -133,17 +137,11 @@ def _fan(g, topo, core, src, dests, aps, remote_sem, local_sem):
     return _bits(m)
 
 
-def _identity(g, T):
-    g.wait_ge(T.sem.ones, 1)
-    g.affine_select(T.ident[:], T.ones[:], [[-1, C]], AluOpType.is_equal, 0.0, 0, 1).then_inc(T.sem.idn, 1)
-
-
 def _rank_core(g, core, T, topo, p, s, j):
     V, PE, SC, SY, sem = g.vector, g.tensor, g.scalar, g.sync, T.sem
     grp = p["groups"][s]
     X0 = T.xs[:, 0:C]
     SY.dma_start(X0, T.x[:]).then_inc(sem.ld, 16)
-    V.memset(T.ones[:], 1.0).then_inc(sem.ones, 1)
 
     V.wait_ge(sem.ld, 16)
     V.tensor_reduce(T.rs[:, 0:1], X0, axis=AxisListType.X, op=AluOpType.add).then_inc(sem.rs, 1)
@@ -174,8 +172,8 @@ def _rank_core(g, core, T, topo, p, s, j):
         if jj != j:
             sent += block_to(jj)
 
-    _identity(g, T)
-    PE.wait_ge(sem.idn, 1)
+    nid = _bits(_ident_mask(topo, p, s, j))
+    PE.wait_ge(sem.idr, nid)
     PE.transpose(T.pt0[:, 0:C], X0, T.ident[:]).then_inc(sem.t0, 1)
     SC.wait_ge(sem.t0, 1)
     SC.activation(T.xt[:, 0:C], T.pt0[:, 0:C], ActivationFunctionType.Copy).then_inc(sem.xt0, 1)
@@ -183,7 +181,7 @@ def _rank_core(g, core, T, topo, p, s, j):
     n = sum(_bits(_fan_mask(topo, p["helper"][p["groups"][t][j]], _last_dests(p, t, j))) for t in range(S))
     a3 = T.land3[:, 2 * s + 1:2 * s + 2]
     PY = [T.py, T.pr0]
-    V.wait_ge(sem.idn, 1)
+    V.wait_ge(sem.idr, nid)
     V.wait_ge(sem.arr3, n)
     V.tensor_reduce(T.cs[:, 0:1], T.land3[:, 0:2 * S:2], axis=AxisListType.X, op=AluOpType.add).then_inc(sem.cs4, 1)
     V.wait_ge(sem.cs4, 1)
@@ -218,7 +216,14 @@ def _helper_core(g, core, T, topo, p, s, j):
     sent = 0
 
     V.memset(T.ones[:], 1.0).then_inc(sem.ones, 1)
-    _identity(g, T)
+    g.wait_ge(sem.ones, 1)
+    g.affine_select(T.ident[:], T.ones[:], [[-1, C]], AluOpType.is_equal, 0.0, 0, 1).then_inc(sem.idn, 1)
+    g.wait_ge(sem.idn, 1)
+    rid, pid = topo.addr(p["cores"][grp[j]], core)
+    mid = _ident_mask(topo, p, s, j)
+    g.remote_dma(out_ap=T.ident[:], in_ap=T.ident[:], remote_sem=sem.idr, local_sem=sem.loc,
+                 pid=pid, routing_id=rid, dma_engine_mask=mid)
+    sent += _bits(mid)
 
     def a_col(k, r):
         if r == 3 and k == 0:

@@ -7,18 +7,16 @@ Q = 2
 S = NR // Q
 C = 128
 H = C // 2
-ON_ENGINES = 4
 
 SCRATCH = {
     "xs": ("sbuf", [128, Q * C], "float32"),
     "xt": ("sbuf", [128, Q * C], "float32"),
-    "ones": ("sbuf", [128, C], "float32"),
+    "ones": ("sbuf", [128, H], "float32"),
     "ident": ("sbuf", [128, C], "float32"),
     "dg": ("sbuf", [128, C], "float32"),
     "yo": ("sbuf", [128, C], "float32"),
     "c1": ("sbuf", [128, 1], "float32"),
-    "land0": ("sbuf", [128, Q], "float32"),
-    "land1": ("sbuf", [128, 4 * S], "float32"),
+    "land1": ("sbuf", [128, NR], "float32"),
     "land2": ("sbuf", [128, 4 * S], "float32"),
     "land3": ("sbuf", [128, 2 * S], "float32"),
     "snd3": ("sbuf", [128, 2], "float32"),
@@ -35,7 +33,7 @@ SCRATCH = {
 }
 SEMAPHORES = (
     ["ld", "st", "ones", "idn", "idr", "loc", "arr0", "arr1", "arr2", "arr3", "rs", "cs4", "b4", "dg0", "dg1",
-     "py0", "py1", "yos"]
+     "py0", "py1", "yo0", "yo1", "st0"]
     + ["%s%d" % (n, k) for n in ("x", "t", "xt") for k in range(Q)]
     + ["%s%d" % (n, r) for n in ("cs", "b", "pc", "snd") for r in (1, 2, 3)]
     + ["%s%d_%d" % (n, k, r) for n in ("r", "a") for k in range(Q) for r in (1, 2, 3)]
@@ -46,17 +44,6 @@ _CACHE = {}
 
 def _bits(m):
     return bin(m).count("1")
-
-
-def _take(m, n):
-    out = 0
-    e = 0
-    while n and (m >> e):
-        if (m >> e) & 1:
-            out |= 1 << e
-            n -= 1
-        e += 1
-    return out
 
 
 def _plan(T, topo):
@@ -99,7 +86,7 @@ def _block_masks(topo, p, s, i):
         if j != i:
             masks[j] = topo.mask(c0, p["helper"][grp[j]])
             off |= masks[j]
-    masks[i] = _take(topo.mask(c0, p["helper"][grp[i]]) & ~off, ON_ENGINES)
+    masks[i] = topo.mask(c0, p["helper"][grp[i]]) & ~off
     return masks
 
 
@@ -115,25 +102,57 @@ def _last_dests(p, s, j):
     return [p["cores"][p["groups"][t][j]] for t in range(S)]
 
 
-def _fan_mask(topo, src, dests):
+def _same_chip(topo, a, b):
+    return topo.host(a) == topo.host(b) and topo.chip(a) == topo.chip(b)
+
+
+def _and_mask(topo, src, dests):
     m = topo.mask(src, dests[0])
     for d in dests:
         m &= topo.mask(src, d)
     return m
 
 
-def _ident_mask(topo, p, s, j):
-    return _fan_mask(topo, p["helper"][p["groups"][s][j]], _mid_dests(p, s, j) + _last_dests(p, s, j))
+def _fan_parts(topo, src, dests):
+    off = [i for i, d in enumerate(dests) if not _same_chip(topo, src, d)]
+    on = [i for i, d in enumerate(dests) if _same_chip(topo, src, d)]
+    if not off or not on:
+        return [(_and_mask(topo, src, dests), off + on)]
+    m_off = _and_mask(topo, src, [dests[i] for i in off])
+    m_on = _and_mask(topo, src, [dests[i] for i in on]) & ~m_off
+    return [(m_off, off), (m_on, on)]
+
+
+def _lands(topo, src, dests, dst):
+    return sum(_bits(m) for m, idx in _fan_parts(topo, src, dests) for i in idx if dests[i] == dst)
 
 
 def _fan(g, topo, core, src, dests, aps, remote_sem, local_sem):
-    m = _fan_mask(topo, core, dests)
-    where = []
-    for d in dests:
-        rid, pid = topo.addr(d, core)
-        where.append(DstId(rid=rid, pnc=pid))
-    g.remote_dma_fused([RemoteDMATransfer(dst_ids=where, dma_engine_mask=m, remote_sem=remote_sem,
-                                          srcs=[src], dsts=aps, alu_op=0)], local_sem=local_sem)
+    trs = []
+    sent = 0
+    for m, idx in _fan_parts(topo, core, dests):
+        where = []
+        for i in idx:
+            rid, pid = topo.addr(dests[i], core)
+            where.append(DstId(rid=rid, pnc=pid))
+        trs.append(RemoteDMATransfer(dst_ids=where, dma_engine_mask=m, remote_sem=remote_sem,
+                                     srcs=[src], dsts=[aps[i] for i in idx], alu_op=0))
+        sent += _bits(m)
+    g.remote_dma_fused(trs, local_sem=local_sem)
+    return sent
+
+
+def _ident_half(g, core, T, topo, mine, peer):
+    V, sem = g.vector, T.sem
+    half = T.ident[:, mine * H:(mine + 1) * H]
+    V.memset(T.ones[:], 1.0).then_inc(sem.ones, 1)
+    g.wait_ge(sem.ones, 1)
+    g.affine_select(half, T.ones[:], [[-1, H]], AluOpType.is_equal, 0.0, -mine * H, 1).then_inc(sem.idn, 1)
+    g.wait_ge(sem.idn, 1)
+    rid, pid = topo.addr(peer, core)
+    m = topo.mask(core, peer)
+    g.remote_dma(out_ap=half, in_ap=half, remote_sem=sem.idr, local_sem=sem.loc, pid=pid, routing_id=rid,
+                 dma_engine_mask=m)
     return _bits(m)
 
 
@@ -142,6 +161,7 @@ def _rank_core(g, core, T, topo, p, s, j):
     grp = p["groups"][s]
     X0 = T.xs[:, 0:C]
     SY.dma_start(X0, T.x[:]).then_inc(sem.ld, 16)
+    sent = _ident_half(g, core, T, topo, 0, p["helper"][grp[j]])
 
     V.wait_ge(sem.ld, 16)
     V.tensor_reduce(T.rs[:, 0:1], X0, axis=AxisListType.X, op=AluOpType.add).then_inc(sem.rs, 1)
@@ -154,7 +174,6 @@ def _rank_core(g, core, T, topo, p, s, j):
     V.tensor_copy(T.c1[:, 0:1], T.pc[:, 0:1]).then_inc(sem.snd1, 1)
 
     masks = _block_masks(topo, p, s, j)
-    sent = 0
 
     def block_to(jj):
         k = 0 if jj == j else 1
@@ -164,23 +183,24 @@ def _rank_core(g, core, T, topo, p, s, j):
         return _bits(masks[jj])
 
     g.wait_ge(sem.ld, 16)
-    sent += block_to(j)
     g.wait_ge(sem.snd1, 1)
     dests = _site_helpers(p, s)
-    sent += _fan(g, topo, core, T.c1[:, 0:1], dests, [T.land0[:, j:j + 1] for _ in dests], sem.arr0, sem.loc)
-    for jj in range(len(grp)):
-        if jj != j:
-            sent += block_to(jj)
+    sent += _fan(g, topo, core, T.c1[:, 0:1], dests, [T.land1[:, Q * s + j:Q * s + j + 1] for _ in dests],
+                 sem.arr0, sem.loc)
+    for jj in [j] + [i for i in range(len(grp)) if i != j]:
+        sent += block_to(jj)
 
-    nid = _bits(_ident_mask(topo, p, s, j))
+    nid = _bits(topo.mask(p["helper"][grp[j]], core))
+    PE.wait_ge(sem.idn, 1)
     PE.wait_ge(sem.idr, nid)
     PE.transpose(T.pt0[:, 0:C], X0, T.ident[:]).then_inc(sem.t0, 1)
     SC.wait_ge(sem.t0, 1)
     SC.activation(T.xt[:, 0:C], T.pt0[:, 0:C], ActivationFunctionType.Copy).then_inc(sem.xt0, 1)
 
-    n = sum(_bits(_fan_mask(topo, p["helper"][p["groups"][t][j]], _last_dests(p, t, j))) for t in range(S))
+    n = sum(_lands(topo, p["helper"][p["groups"][t][j]], _last_dests(p, t, j), core) for t in range(S))
     a3 = T.land3[:, 2 * s + 1:2 * s + 2]
     PY = [T.py, T.pr0]
+    V.wait_ge(sem.idn, 1)
     V.wait_ge(sem.idr, nid)
     V.wait_ge(sem.arr3, n)
     V.tensor_reduce(T.cs[:, 0:1], T.land3[:, 0:2 * S:2], axis=AxisListType.X, op=AluOpType.add).then_inc(sem.cs4, 1)
@@ -196,9 +216,13 @@ def _rank_core(g, core, T, topo, p, s, j):
             sem["py%d" % h], 1)
     for h in (0, 1):
         V.wait_ge(sem["py%d" % h], 1)
-        V.tensor_scalar(T.yo[:, h * H:(h + 1) * H], PY[h][:, 0:H], a3, None, AluOpType.mult).then_inc(sem.yos, 1)
-    SY.wait_ge(sem.yos, 2)
-    SY.dma_start(T.y[:], T.yo[:]).then_inc(sem.st, 16)
+        V.tensor_scalar(T.yo[:, h * H:(h + 1) * H], PY[h][:, 0:H], a3, None, AluOpType.mult).then_inc(
+            sem["yo%d" % h], 1)
+    SC.wait_ge(sem.yo0, 1)
+    SC.dma_start(T.y[:, 0:H], T.yo[:, 0:H]).then_inc(sem.st0, 16)
+    SY.wait_ge(sem.yo1, 1)
+    SY.dma_start(T.y[:, H:C], T.yo[:, H:C]).then_inc(sem.st, 16)
+    SC.wait_ge(sem.st0, 16)
     SY.wait_ge(sem.st, 16)
     g.wait_ge(sem.loc, sent)
 
@@ -213,32 +237,22 @@ def _helper_core(g, core, T, topo, p, s, j):
     PT = [T["pt%d" % k] for k in range(nb)]
     member = [j] + [i for i in range(nb) if i != j]
     nx = [_bits(_block_masks(topo, p, s, member[k])[j]) for k in range(nb)]
-    sent = 0
-
-    V.memset(T.ones[:], 1.0).then_inc(sem.ones, 1)
-    g.wait_ge(sem.ones, 1)
-    g.affine_select(T.ident[:], T.ones[:], [[-1, C]], AluOpType.is_equal, 0.0, 0, 1).then_inc(sem.idn, 1)
-    g.wait_ge(sem.idn, 1)
-    rid, pid = topo.addr(p["cores"][grp[j]], core)
-    mid = _ident_mask(topo, p, s, j)
-    g.remote_dma(out_ap=T.ident[:], in_ap=T.ident[:], remote_sem=sem.idr, local_sem=sem.loc,
-                 pid=pid, routing_id=rid, dma_engine_mask=mid)
-    sent += _bits(mid)
+    sent = _ident_half(g, core, T, topo, 1, p["cores"][grp[j]])
+    nid = _bits(topo.mask(p["cores"][grp[j]], core))
 
     def a_col(k, r):
         if r == 3 and k == 0:
             return T.snd3[:, 1:2]
         return T.av[:, 2 * (r - 1) + k:2 * (r - 1) + k + 1]
 
-    n0 = sum(_bits(_fan_mask(topo, p["cores"][r], _site_helpers(p, s))) for r in grp)
-    out = T.land1[:, 4 * s:4 * s + 1]
-    V.wait_ge(sem.arr0, n0)
-    V.tensor_reduce(out, T.land0[:, 0:nb], axis=AxisListType.X, op=AluOpType.add).then_inc(sem.snd1, 1)
-    g.wait_ge(sem.snd1, 1)
+    n0 = sum(_lands(topo, p["cores"][r], _site_helpers(p, s), core) for r in grp)
+    out = T.land1[:, Q * s:Q * s + nb]
+    g.wait_ge(sem.arr0, n0)
     dests = _mid_dests(p, s, j)
     sent += _fan(g, topo, core, out, dests, [out for _ in dests], sem.arr1, sem.loc)
 
     PE.wait_ge(sem.idn, 1)
+    PE.wait_ge(sem.idr, nid)
     for k in range(nb):
         PE.wait_ge(sem["x%d" % k], nx[k])
         PE.transpose(PT[k][:, 0:C], X[k], T.ident[:]).then_inc(sem["t%d" % k], 1)
@@ -246,12 +260,15 @@ def _helper_core(g, core, T, topo, p, s, j):
         SC.activation(XT[k], PT[k][:, 0:C], ActivationFunctionType.Copy).then_inc(sem["xt%d" % k], 1)
 
     for r in (2, 3):
-        land = T["land%d" % (r - 1)]
-        n = sum(_bits(_fan_mask(topo, p["helper"][p["groups"][t][j]], _mid_dests(p, t, j)))
+        land = T.land1[:, 0:NR] if r == 2 else T.land2[:, 0:4 * S:4]
+        n = sum(_lands(topo, p["helper"][p["groups"][t][j]], _mid_dests(p, t, j), core)
                 for t in range(S) if t != s)
         V.wait_ge(sem["arr%d" % (r - 1)], n)
-        V.wait_ge(sem["snd%d" % (r - 1)], 1)
-        V.tensor_reduce(T.cs[:, r:r + 1], land[:, 0:4 * S:4], axis=AxisListType.X, op=AluOpType.add).then_inc(
+        if r == 2:
+            V.wait_ge(sem.arr0, n0)
+        else:
+            V.wait_ge(sem["snd%d" % (r - 1)], 1)
+        V.tensor_reduce(T.cs[:, r:r + 1], land, axis=AxisListType.X, op=AluOpType.add).then_inc(
             sem["cs%d" % r], 1)
         V.wait_ge(sem["cs%d" % r], 1)
         V.reciprocal(T.bv[:, r:r + 1], T.cs[:, r:r + 1]).then_inc(sem["b%d" % r], 1)

from concourse.bass import DstId, RemoteDMATransfer
from concourse.mybir import AluOpType, AxisListType, ActivationFunctionType

NSIM = 256
NR = 10
Q = 2
S = NR // Q
C = 128
H = C // 2

SCRATCH = {
    "xs": ("sbuf", [128, Q * C], "float32"),
    "xt": ("sbuf", [128, Q * C], "float32"),
    "ones": ("sbuf", [128, H], "float32"),
    "ident": ("sbuf", [128, C], "float32"),
    "dg": ("sbuf", [128, C], "float32"),
    "yo": ("sbuf", [128, C], "float32"),
    "c1": ("sbuf", [128, 1], "float32"),
    "land1": ("sbuf", [128, NR], "float32"),
    "land2": ("sbuf", [128, 4 * S], "float32"),
    "land3": ("sbuf", [128, 2 * S], "float32"),
    "snd3": ("sbuf", [128, 2], "float32"),
    "rs": ("sbuf", [128, 4], "float32"),
    "av": ("sbuf", [128, 8], "float32"),
    "cs": ("sbuf", [128, 4], "float32"),
    "bv": ("sbuf", [128, 4], "float32"),
    "pc": ("psum", [128, 512], "float32"),
    "pr0": ("psum", [128, 512], "float32"),
    "pr1": ("psum", [128, 512], "float32"),
    "pt0": ("psum", [128, 512], "float32"),
    "pt1": ("psum", [128, 512], "float32"),
    "py": ("psum", [128, 512], "float32"),
}
SEMAPHORES = (
    ["ld", "st", "ones", "idn", "idr", "loc", "arr0", "arr1", "arr2", "arr3", "rs", "cs4", "b4", "dg0", "dg1",
     "py0", "py1", "yo0", "yo1", "st0"]
    + ["%s%d" % (n, k) for n in ("x", "t", "xt") for k in range(Q)]
    + ["%s%d" % (n, r) for n in ("cs", "b", "pc", "snd") for r in (1, 2, 3)]
    + ["%s%d_%d" % (n, k, r) for n in ("r", "a") for k in range(Q) for r in (1, 2, 3)]
)

_CACHE = {}


def _bits(m):
    return bin(m).count("1")


def _plan(T, topo):
    if "p" in _CACHE:
        return _CACHE["p"]
    cores = [int(c) for c in T.cores]
    left = list(range(len(cores)))
    groups = []
    while left:
        i = left.pop(0)
        grp = [i]
        for k in list(left):
            if len(grp) < Q and topo.same_plane(cores[i], cores[k]):
                grp.append(k)
                left.remove(k)
        groups.append(grp)
    helper = {}
    for r, c in enumerate(cores):
        cand = [w for w in range(NSIM)
                if w not in cores and topo.host(w) == topo.host(c) and topo.chip(w) == topo.chip(c)
                and all(topo.may_write(w, d) for d in cores)]
        cand.sort(key=lambda w: (topo.die(w) != topo.die(c), w))
        helper[r] = cand[0]
    role = {}
    for s, grp in enumerate(groups):
        for j, r in enumerate(grp):
            role[cores[r]] = ("rank", s, j)
            role[helper[r]] = ("help", s, j)
    p = {"cores": cores, "groups": groups, "helper": helper, "role": role}
    _CACHE["p"] = p
    return p


def _block_masks(topo, p, s, i):
    grp = p["groups"][s]
    c0 = p["cores"][grp[i]]
    off = 0
    masks = {}
    for j in range(len(grp)):
        if j != i:
            masks[j] = topo.mask(c0, p["helper"][grp[j]])
            off |= masks[j]
    masks[i] = topo.mask(c0, p["helper"][grp[i]]) & ~off
    return masks


def _site_helpers(p, s):
    return [p["helper"][r] for r in p["groups"][s]]


def _mid_dests(p, s, j):
    return [p["helper"][p["groups"][t][j]] for t in range(S) if t != s]


def _last_dests(p, s, j):
    return [p["cores"][p["groups"][t][j]] for t in range(S)]


def _same_chip(topo, a, b):
    return topo.host(a) == topo.host(b) and topo.chip(a) == topo.chip(b)


def _and_mask(topo, src, dests):
    m = topo.mask(src, dests[0])
    for d in dests:
        m &= topo.mask(src, d)
    return m


def _fan_parts(topo, src, dests):
    off = [i for i, d in enumerate(dests) if not _same_chip(topo, src, d)]
    on = [i for i, d in enumerate(dests) if _same_chip(topo, src, d)]
    if not off or not on:
        return [(_and_mask(topo, src, dests), off + on)]
    m_off = _and_mask(topo, src, [dests[i] for i in off])
    m_on = _and_mask(topo, src, [dests[i] for i in on]) & ~m_off
    return [(m_off, off), (m_on, on)]


def _lands(topo, src, dests, dst):
    return sum(_bits(m) for m, idx in _fan_parts(topo, src, dests) for i in idx if dests[i] == dst)


def _fan(g, topo, core, src, dests, aps, remote_sem, local_sem):
    trs = []
    sent = 0
    for m, idx in _fan_parts(topo, core, dests):
        where = []
        for i in idx:
            rid, pid = topo.addr(dests[i], core)
            where.append(DstId(rid=rid, pnc=pid))
        trs.append(RemoteDMATransfer(dst_ids=where, dma_engine_mask=m, remote_sem=remote_sem,
                                     srcs=[src], dsts=[aps[i] for i in idx], alu_op=0))
        sent += _bits(m)
    g.remote_dma_fused(trs, local_sem=local_sem)
    return sent


def _ident_half(g, core, T, topo, mine, peer):
    V, sem = g.vector, T.sem
    half = T.ident[:, mine * H:(mine + 1) * H]
    V.memset(T.ones[:], 1.0).then_inc(sem.ones, 1)
    g.wait_ge(sem.ones, 1)
    g.affine_select(half, T.ones[:], [[-1, H]], AluOpType.is_equal, 0.0, -mine * H, 1).then_inc(sem.idn, 1)
    g.wait_ge(sem.idn, 1)
    rid, pid = topo.addr(peer, core)
    m = topo.mask(core, peer)
    g.remote_dma(out_ap=half, in_ap=half, remote_sem=sem.idr, local_sem=sem.loc, pid=pid, routing_id=rid,
                 dma_engine_mask=m)
    return _bits(m)


def _rank_core(g, core, T, topo, p, s, j):
    V, PE, SC, SY, sem = g.vector, g.tensor, g.scalar, g.sync, T.sem
    grp = p["groups"][s]
    X0 = T.xs[:, 0:C]
    SY.dma_start(X0, T.x[:]).then_inc(sem.ld, 16)
    sent = _ident_half(g, core, T, topo, 0, p["helper"][grp[j]])

    V.wait_ge(sem.ld, 16)
    V.tensor_reduce(T.rs[:, 0:1], X0, axis=AxisListType.X, op=AluOpType.add).then_inc(sem.rs, 1)
    V.wait_ge(sem.rs, 1)
    V.reciprocal(T.av[:, 0:1], T.rs[:, 0:1]).then_inc(sem["a0_1"], 1)
    PE.wait_ge(sem.ld, 16)
    PE.wait_ge(sem["a0_1"], 1)
    PE.matmul(T.pc[:, 0:1], X0, T.av[:, 0:1], start=True, stop=True).then_inc(sem.pc1, 1)
    V.wait_ge(sem.pc1, 1)
    V.tensor_copy(T.c1[:, 0:1], T.pc[:, 0:1]).then_inc(sem.snd1, 1)

    masks = _block_masks(topo, p, s, j)

    def block_to(jj):
        k = 0 if jj == j else 1
        rid, pid = topo.addr(p["helper"][grp[jj]], core)
        g.remote_dma(out_ap=T.xs[:, k * C:(k + 1) * C], in_ap=X0, remote_sem=sem["x%d" % k], local_sem=sem.loc,
                     pid=pid, routing_id=rid, dma_engine_mask=masks[jj])
        return _bits(masks[jj])

    g.wait_ge(sem.ld, 16)
    g.wait_ge(sem.snd1, 1)
    dests = _site_helpers(p, s)
    sent += _fan(g, topo, core, T.c1[:, 0:1], dests, [T.land1[:, Q * s + j:Q * s + j + 1] for _ in dests],
                 sem.arr0, sem.loc)
    for jj in [j] + [i for i in range(len(grp)) if i != j]:
        sent += block_to(jj)

    nid = _bits(topo.mask(p["helper"][grp[j]], core))
    PE.wait_ge(sem.idn, 1)
    PE.wait_ge(sem.idr, nid)
    PE.transpose(T.pt0[:, 0:C], X0, T.ident[:]).then_inc(sem.t0, 1)
    SC.wait_ge(sem.t0, 1)
    SC.activation(T.xt[:, 0:C], T.pt0[:, 0:C], ActivationFunctionType.Copy).then_inc(sem.xt0, 1)

    n = sum(_lands(topo, p["helper"][p["groups"][t][j]], _last_dests(p, t, j), core) for t in range(S))
    a3 = T.land3[:, 2 * s + 1:2 * s + 2]
    PY = [T.py, T.pr0]
    V.wait_ge(sem.idn, 1)
    V.wait_ge(sem.idr, nid)
    V.wait_ge(sem.arr3, n)
    V.tensor_reduce(T.cs[:, 0:1], T.land3[:, 0:2 * S:2], axis=AxisListType.X, op=AluOpType.add).then_inc(sem.cs4, 1)
    V.wait_ge(sem.cs4, 1)
    V.reciprocal(T.bv[:, 0:1], T.cs[:, 0:1]).then_inc(sem.b4, 1)
    V.wait_ge(sem.b4, 1)
    PE.wait_ge(sem.xt0, 1)
    for h in (0, 1):
        V.tensor_scalar(T.dg[:, h * H:(h + 1) * H], T.ident[:, h * H:(h + 1) * H], T.bv[:, 0:1], None,
                        AluOpType.mult).then_inc(sem["dg%d" % h], 1)
        PE.wait_ge(sem["dg%d" % h], 1)
        PE.matmul(PY[h][:, 0:H], T.xt[:, 0:C], T.dg[:, h * H:(h + 1) * H], start=True, stop=True).then_inc(
            sem["py%d" % h], 1)
    for h in (0, 1):
        V.wait_ge(sem["py%d" % h], 1)
        V.tensor_scalar(T.yo[:, h * H:(h + 1) * H], PY[h][:, 0:H], a3, None, AluOpType.mult).then_inc(
            sem["yo%d" % h], 1)
    SC.wait_ge(sem.yo0, 1)
    SC.dma_start(T.y[:, 0:H], T.yo[:, 0:H]).then_inc(sem.st0, 16)
    SY.wait_ge(sem.yo1, 1)
    SY.dma_start(T.y[:, H:C], T.yo[:, H:C]).then_inc(sem.st, 16)
    SC.wait_ge(sem.st0, 16)
    SY.wait_ge(sem.st, 16)
    g.wait_ge(sem.loc, sent)


def _helper_core(g, core, T, topo, p, s, j):
    V, PE, SC, sem = g.vector, g.tensor, g.scalar, T.sem
    grp = p["groups"][s]
    nb = len(grp)
    X = [T.xs[:, k * C:(k + 1) * C] for k in range(nb)]
    XT = [T.xt[:, k * C:(k + 1) * C] for k in range(nb)]
    PR = [T["pr%d" % k] for k in range(nb)]
    PT = [T["pt%d" % k] for k in range(nb)]
    member = [j] + [i for i in range(nb) if i != j]
    nx = [_bits(_block_masks(topo, p, s, member[k])[j]) for k in range(nb)]
    sent = _ident_half(g, core, T, topo, 1, p["cores"][grp[j]])
    nid = _bits(topo.mask(p["cores"][grp[j]], core))

    def a_col(k, r):
        if r == 3 and k == 0:
            return T.snd3[:, 1:2]
        return T.av[:, 2 * (r - 1) + k:2 * (r - 1) + k + 1]

    n0 = sum(_lands(topo, p["cores"][r], _site_helpers(p, s), core) for r in grp)
    out = T.land1[:, Q * s:Q * s + nb]
    g.wait_ge(sem.arr0, n0)
    dests = _mid_dests(p, s, j)
    sent += _fan(g, topo, core, out, dests, [out for _ in dests], sem.arr1, sem.loc)

    PE.wait_ge(sem.idn, 1)
    PE.wait_ge(sem.idr, nid)
    for k in range(nb):
        PE.wait_ge(sem["x%d" % k], nx[k])
        PE.transpose(PT[k][:, 0:C], X[k], T.ident[:]).then_inc(sem["t%d" % k], 1)
        SC.wait_ge(sem["t%d" % k], 1)
        SC.activation(XT[k], PT[k][:, 0:C], ActivationFunctionType.Copy).then_inc(sem["xt%d" % k], 1)

    for r in (2, 3):
        land = T.land1[:, 0:NR] if r == 2 else T.land2[:, 0:4 * S:4]
        n = sum(_lands(topo, p["helper"][p["groups"][t][j]], _mid_dests(p, t, j), core)
                for t in range(S) if t != s)
        V.wait_ge(sem["arr%d" % (r - 1)], n)
        if r == 2:
            V.wait_ge(sem.arr0, n0)
        else:
            V.wait_ge(sem["snd%d" % (r - 1)], 1)
        V.tensor_reduce(T.cs[:, r:r + 1], land, axis=AxisListType.X, op=AluOpType.add).then_inc(
            sem["cs%d" % r], 1)
        V.wait_ge(sem["cs%d" % r], 1)
        V.reciprocal(T.bv[:, r:r + 1], T.cs[:, r:r + 1]).then_inc(sem["b%d" % r], 1)
        PE.wait_ge(sem["b%d" % r], 1)
        for k in range(nb):
            PE.wait_ge(sem["xt%d" % k], 1)
            PE.matmul(PR[k][:, r:r + 1], XT[k], T.bv[:, r:r + 1], start=True, stop=True).then_inc(
                sem["r%d_%d" % (k, r)], 1)
        for k in range(nb):
            V.wait_ge(sem["r%d_%d" % (k, r)], 1)
            V.reciprocal(a_col(k, r), PR[k][:, r:r + 1]).then_inc(sem["a%d_%d" % (k, r)], 1)

        for k in range(nb):
            PE.wait_ge(sem["a%d_%d" % (k, r)], 1)
            mm = PE.matmul(T.pc[:, r:r + 1], X[k], a_col(k, r), start=(k == 0), stop=(k == nb - 1))
        mm.then_inc(sem["pc%d" % r], 1)
        V.wait_ge(sem["pc%d" % r], 1)
        if r < 3:
            out = T["land%d" % r][:, 4 * s:4 * s + 1]
            V.tensor_copy(out, T.pc[:, r:r + 1]).then_inc(sem["snd%d" % r], 1)
            g.wait_ge(sem["snd%d" % r], 1)
            dests = _mid_dests(p, s, j)
            sent += _fan(g, topo, core, out, dests, [out for _ in dests], sem["arr%d" % r], sem.loc)
        else:
            V.tensor_copy(T.snd3[:, 0:1], T.pc[:, r:r + 1]).then_inc(sem["snd%d" % r], 1)
            g.wait_ge(sem["snd%d" % r], 1)
            g.wait_ge(sem["a0_%d" % r], 1)
            dests = _last_dests(p, s, j)
            sent += _fan(g, topo, core, T.snd3[:], dests, [T.land3[:, 2 * s:2 * s + 2] for _ in dests],
                         sem.arr3, sem.loc)

    g.wait_ge(sem.loc, sent)


def rank_program(g, core, T, topo):
    p = _plan(T, topo)
    if core not in p["role"]:
        return
    kind, s, j = p["role"][core]
    if kind == "rank":
        _rank_core(g, core, T, topo, p, s, j)
    else:
        _helper_core(g, core, T, topo, p, s, j)
